import numpy as np, ml_dtypes
CORES = [30,158,46,174,86,214]
N = 6
R = 512
def setup_inputs(rng):
    m = (rng.standard_normal((N, 128, 128), dtype=np.float32) / 11).astype(ml_dtypes.bfloat16)
    q = rng.standard_normal((128, R), dtype=np.float32).astype(ml_dtypes.bfloat16)
    return {"m": m, "mt": m.transpose(0, 2, 1).copy(), "q": np.broadcast_to(q, (N, 128, R)).copy()}
def setup_inputs_big(rng):
    d = setup_inputs(rng)
    for k in ("m", "mt", "q"): d[k] = (d[k].astype(np.float32) * 1024.0).astype(d[k].dtype)
    return d
def setup_inputs_small(rng):
    d = setup_inputs(rng)
    for k in ("m", "mt", "q"): d[k] = (d[k].astype(np.float32) * (1 / 1024.0)).astype(d[k].dtype)
    return d
def setup_inputs_apart(rng):
    d = setup_inputs(rng)
    f = (10.0 ** rng.permutation(np.linspace(-1.5, 1.5, N))).astype(np.float32).reshape(N, 1, 1)
    for k in ("m", "mt"): d[k] = (d[k].astype(np.float32) * f).astype(d[k].dtype)
    return d
def tie_inputs(x):
    x = dict(x)
    x["mt"] = x["m"].transpose(0, 2, 1).copy(); x["q"] = np.broadcast_to(x["q"][0], x["q"].shape).copy()
    return x
def reference(m, mt, q):
    M, MT, Q = m.astype(np.float64), mt.astype(np.float64), q.astype(np.float64)
    p = sum(MT[j].T @ Q[j] for j in range(N))
    q2 = sum(M[j].T @ p for j in range(N))
    return {"p": np.broadcast_to(p.astype(ml_dtypes.bfloat16 if m.dtype != np.float64 else np.float64), (N, 128, R)), "q2": np.broadcast_to(q2.astype(ml_dtypes.bfloat16 if m.dtype != np.float64 else np.float64), (N, 128, R))}

@@ -1,0 +1,112 @@
+from concourse.bass import DstId, RemoteDMATransfer
+
+W = 128
+R = 512
+H = R // 2
+N = 6
+
+SCRATCH = {
+    "land": ("sbuf", [128, N * W], "bfloat16"),
+    "qs": ("sbuf", [128, R], "bfloat16"),
+    "z": ("sbuf", [128, W + 1], "bfloat16"),
+    "zd": ("dram", [W + 1, 128], "bfloat16"),
+    "eye": ("sbuf", [128, W], "bfloat16"),
+    "st": ("sbuf", [128, W], "bfloat16"),
+    "s": ("sbuf", [128, W], "bfloat16"),
+    "ps": ("sbuf", [128, R], "bfloat16"),
+    "q2s": ("sbuf", [128, R], "bfloat16"),
+    "acc_st": ("psum", [128, 512], "float32"),
+    "acc_s": ("psum", [128, 512], "float32"),
+    "acc_pa": ("psum", [128, 512], "float32"),
+    "acc_pb": ("psum", [128, 512], "float32"),
+    "acc_qa": ("psum", [128, 512], "float32"),
+    "acc_qb": ("psum", [128, 512], "float32"),
+}
+SEMAPHORES = ["ld_mt", "ld_q", "fill", "id1", "id2", "sent",
+              "m_st", "m_s", "m_pa", "m_pb", "m_qa", "m_qb",
+              "c_st", "c_s", "c_pa", "c_pb", "c_qa", "c_qb",
+              "out_a", "out_b"] + ["arr%d" % j for j in range(N)]
+
+
+def rank_program(g, core, T, topo):
+    rank = T.rank_of(core)
+    if rank is None:
+        return
+    n = len(T.cores)
+    sem = T.sem
+    own = T.land[:, rank * W:(rank + 1) * W]
+    te, ve, sy, sc = g.tensor, g.vector, g.sync, g.scalar
+
+    sy.dma_start(own, T.mt[:, :]).then_inc(sem.ld_mt, 16)
+    sy.dma_start(T.qs[:, :], T.q[:, :]).then_inc(sem.ld_q, 16)
+
+    ve.memset(T.z[:, 0:1], 1.0).then_inc(sem.fill, 1)
+    ve.memset(T.z[:, 1:W + 1], 0.0).then_inc(sem.fill, 1)
+    sc.wait_ge(sem.fill, 2)
+    sc.dma_start(T.zd[:, :], T.z[:, :]).then_inc(sem.id1, 16)
+    sc.wait_ge(sem.id1, 16)
+    sc.dma_start(T.eye[:, :], T.zd[0:W, :]).then_inc(sem.id2, 16)
+
+    peers = [T.cores[(rank + k) % n] for k in range(1, n)]
+    mask = topo.mask(core, peers[0])
+    for d in peers:
+        mask &= topo.mask(core, d)
+    ne = bin(mask).count("1")
+    ids = []
+    for d in peers:
+        rid, pid = topo.addr(d, core)
+        ids.append(DstId(rid=rid, pnc=pid))
+    g.wait_ge(sem.ld_mt, 16)
+    g.remote_dma_fused(
+        [RemoteDMATransfer(dst_ids=ids, dma_engine_mask=mask, remote_sem=sem["arr%d" % rank],
+                           srcs=[own], dsts=[own for _ in peers], alu_op=0)],
+        local_sem=sem.sent)
+
+    te.wait_ge(sem.id2, 16)
+    te.wait_ge(sem.ld_mt, 16)
+    order = [rank] + [(rank - k) % n for k in range(1, n)]
+    for i, j in enumerate(order):
+        if i > 0:
+            te.wait_ge(sem["arr%d" % j], ne)
+        blk = T.land[:, j * W:(j + 1) * W]
+        a = te.matmul(T.acc_st[:, 0:W], T.eye[:, :], blk, i == 0, i == n - 1)
+        b = te.matmul(T.acc_s[:, 0:W], blk, T.eye[:, :], i == 0, i == n - 1)
+        if i == n - 1:
+            a.then_inc(sem.m_st, 1)
+            b.then_inc(sem.m_s, 1)
+    ve.wait_ge(sem.m_st, 1)
+    ve.tensor_copy(T.st[:, :], T.acc_st[:, 0:W]).then_inc(sem.c_st, 1)
+    ve.wait_ge(sem.m_s, 1)
+    ve.tensor_copy(T.s[:, :], T.acc_s[:, 0:W]).then_inc(sem.c_s, 1)
+
+    te.wait_ge(sem.c_st, 1)
+    te.wait_ge(sem.ld_q, 16)
+    te.matmul(T.acc_pa[:, 0:H], T.st[:, :], T.qs[:, 0:H], True, True).then_inc(sem.m_pa, 1)
+    te.matmul(T.acc_pb[:, 0:H], T.st[:, :], T.qs[:, H:R], True, True).then_inc(sem.m_pb, 1)
+    ve.wait_ge(sem.m_pa, 1)
+    ve.tensor_copy(T.ps[:, 0:H], T.acc_pa[:, 0:H]).then_inc(sem.c_pa, 1)
+    ve.wait_ge(sem.m_pb, 1)
+    ve.tensor_copy(T.ps[:, H:R], T.acc_pb[:, 0:H]).then_inc(sem.c_pb, 1)
+
+    te.wait_ge(sem.c_s, 1)
+    te.wait_ge(sem.c_pa, 1)
+    te.matmul(T.acc_qa[:, 0:H], T.s[:, :], T.ps[:, 0:H], True, True).then_inc(sem.m_qa, 1)
+    te.wait_ge(sem.c_pb, 1)
+    te.matmul(T.acc_qb[:, 0:H], T.s[:, :], T.ps[:, H:R], True, True).then_inc(sem.m_qb, 1)
+    ve.wait_ge(sem.m_qa, 1)
+    ve.tensor_copy(T.q2s[:, 0:H], T.acc_qa[:, 0:H]).then_inc(sem.c_qa, 1)
+    ve.wait_ge(sem.m_qb, 1)
+    ve.tensor_copy(T.q2s[:, H:R], T.acc_qb[:, 0:H]).then_inc(sem.c_qb, 1)
+
+    sy.wait_ge(sem.c_pa, 1)
+    sy.dma_start(T.p[:, 0:H], T.ps[:, 0:H]).then_inc(sem.out_a, 16)
+    sc.wait_ge(sem.c_pb, 1)
+    sc.dma_start(T.p[:, H:R], T.ps[:, H:R]).then_inc(sem.out_b, 16)
+    sy.wait_ge(sem.c_qa, 1)
+    sy.dma_start(T.q2[:, 0:H], T.q2s[:, 0:H]).then_inc(sem.out_a, 16)
+    sc.wait_ge(sem.c_qb, 1)
+    sc.dma_start(T.q2[:, H:R], T.q2s[:, H:R]).then_inc(sem.out_b, 16)
+
+    g.wait_ge(sem.sent, ne)
+    sy.wait_ge(sem.out_a, 32)
+    sc.wait_ge(sem.out_b, 32)

@@ -1,15 +1,16 @@
 from concourse.bass import DstId, RemoteDMATransfer
+from concourse.mybir import AluOpType
 
 W = 128
 R = 512
-H = R // 2
+NB = 4
+B = R // NB
 N = 6
 
 SCRATCH = {
     "land": ("sbuf", [128, N * W], "bfloat16"),
     "qs": ("sbuf", [128, R], "bfloat16"),
-    "z": ("sbuf", [128, W + 1], "bfloat16"),
-    "zd": ("dram", [W + 1, 128], "bfloat16"),
+    "ones": ("sbuf", [128, W], "bfloat16"),
     "eye": ("sbuf", [128, W], "bfloat16"),
     "st": ("sbuf", [128, W], "bfloat16"),
     "s": ("sbuf", [128, W], "bfloat16"),
@@ -17,15 +18,17 @@ SCRATCH = {
     "q2s": ("sbuf", [128, R], "bfloat16"),
     "acc_st": ("psum", [128, 512], "float32"),
     "acc_s": ("psum", [128, 512], "float32"),
-    "acc_pa": ("psum", [128, 512], "float32"),
-    "acc_pb": ("psum", [128, 512], "float32"),
-    "acc_qa": ("psum", [128, 512], "float32"),
-    "acc_qb": ("psum", [128, 512], "float32"),
+    "bk0": ("psum", [128, 512], "float32"),
+    "bk1": ("psum", [128, 512], "float32"),
+    "bk2": ("psum", [128, 512], "float32"),
+    "bk3": ("psum", [128, 512], "float32"),
+    "bk4": ("psum", [128, 512], "float32"),
+    "bk5": ("psum", [128, 512], "float32"),
 }
-SEMAPHORES = ["ld_mt", "ld_q", "fill", "id1", "id2", "sent",
-              "m_st", "m_s", "m_pa", "m_pb", "m_qa", "m_qb",
-              "c_st", "c_s", "c_pa", "c_pb", "c_qa", "c_qb",
-              "out_a", "out_b"] + ["arr%d" % j for j in range(N)]
+SEMAPHORES = (["ld_mt", "ld_q", "fill", "id", "sent", "m_st", "m_s", "c_st", "c_s", "out_a", "out_b"]
+              + ["m_p%d" % k for k in range(NB)] + ["c_p%d" % k for k in range(NB)]
+              + ["m_q%d" % k for k in range(NB)] + ["c_q%d" % k for k in range(NB)]
+              + ["arr%d" % j for j in range(N)])
 
 
 def rank_program(g, core, T, topo):
@@ -39,13 +42,7 @@ def rank_program(g, core, T, topo):
 
     sy.dma_start(own, T.mt[:, :]).then_inc(sem.ld_mt, 16)
     sy.dma_start(T.qs[:, :], T.q[:, :]).then_inc(sem.ld_q, 16)
-
-    ve.memset(T.z[:, 0:1], 1.0).then_inc(sem.fill, 1)
-    ve.memset(T.z[:, 1:W + 1], 0.0).then_inc(sem.fill, 1)
-    sc.wait_ge(sem.fill, 2)
-    sc.dma_start(T.zd[:, :], T.z[:, :]).then_inc(sem.id1, 16)
-    sc.wait_ge(sem.id1, 16)
-    sc.dma_start(T.eye[:, :], T.zd[0:W, :]).then_inc(sem.id2, 16)
+    ve.memset(T.ones[:, :], 1.0).then_inc(sem.fill, 1)
 
     peers = [T.cores[(rank + k) % n] for k in range(1, n)]
     mask = topo.mask(core, peers[0])
@@ -62,51 +59,60 @@ def rank_program(g, core, T, topo):
                            srcs=[own], dsts=[own for _ in peers], alu_op=0)],
         local_sem=sem.sent)
 
-    te.wait_ge(sem.id2, 16)
-    te.wait_ge(sem.ld_mt, 16)
+    g.wait_ge(sem.fill, 1)
+    g.affine_select(T.eye[:, :], T.ones[:, :], [[-1, W]], AluOpType.is_equal, 0.0, 0, 1).then_inc(sem.id, 1)
+
     order = [rank] + [(rank - k) % n for k in range(1, n)]
+    last = order[-1]
+    lastblk = T.land[:, last * W:(last + 1) * W]
+    te.wait_ge(sem.id, 1)
+    te.wait_ge(sem.ld_mt, 16)
     for i, j in enumerate(order):
         if i > 0:
             te.wait_ge(sem["arr%d" % j], ne)
         blk = T.land[:, j * W:(j + 1) * W]
-        a = te.matmul(T.acc_st[:, 0:W], T.eye[:, :], blk, i == 0, i == n - 1)
+        if i < n - 1:
+            a = te.matmul(T.acc_st[:, 0:W], T.eye[:, :], blk, i == 0, i == n - 2)
+            if i == n - 2:
+                a.then_inc(sem.m_st, 1)
         b = te.matmul(T.acc_s[:, 0:W], blk, T.eye[:, :], i == 0, i == n - 1)
         if i == n - 1:
-            a.then_inc(sem.m_st, 1)
             b.then_inc(sem.m_s, 1)
+
     ve.wait_ge(sem.m_st, 1)
-    ve.tensor_copy(T.st[:, :], T.acc_st[:, 0:W]).then_inc(sem.c_st, 1)
+    ve.wait_ge(sem["arr%d" % last], ne)
+    ve.tensor_tensor(T.st[:, :], T.acc_st[:, 0:W], lastblk, AluOpType.add).then_inc(sem.c_st, 1)
     ve.wait_ge(sem.m_s, 1)
     ve.tensor_copy(T.s[:, :], T.acc_s[:, 0:W]).then_inc(sem.c_s, 1)
 
+    pbank = [T.bk0, T.bk1, T.bk2, T.bk3]
+    qbank = [T.bk4, T.bk5, T.bk0, T.bk1]
     te.wait_ge(sem.c_st, 1)
     te.wait_ge(sem.ld_q, 16)
-    te.matmul(T.acc_pa[:, 0:H], T.st[:, :], T.qs[:, 0:H], True, True).then_inc(sem.m_pa, 1)
-    te.matmul(T.acc_pb[:, 0:H], T.st[:, :], T.qs[:, H:R], True, True).then_inc(sem.m_pb, 1)
-    ve.wait_ge(sem.m_pa, 1)
-    ve.tensor_copy(T.ps[:, 0:H], T.acc_pa[:, 0:H]).then_inc(sem.c_pa, 1)
-    ve.wait_ge(sem.m_pb, 1)
-    ve.tensor_copy(T.ps[:, H:R], T.acc_pb[:, 0:H]).then_inc(sem.c_pb, 1)
-
+    for k in range(NB):
+        te.matmul(pbank[k][:, 0:B], T.st[:, :], T.qs[:, k * B:(k + 1) * B], True, True).then_inc(sem["m_p%d" % k], 1)
+    for k in range(NB):
+        ve.wait_ge(sem["m_p%d" % k], 1)
+        ve.tensor_copy(T.ps[:, k * B:(k + 1) * B], pbank[k][:, 0:B]).then_inc(sem["c_p%d" % k], 1)
     te.wait_ge(sem.c_s, 1)
-    te.wait_ge(sem.c_pa, 1)
-    te.matmul(T.acc_qa[:, 0:H], T.s[:, :], T.ps[:, 0:H], True, True).then_inc(sem.m_qa, 1)
-    te.wait_ge(sem.c_pb, 1)
-    te.matmul(T.acc_qb[:, 0:H], T.s[:, :], T.ps[:, H:R], True, True).then_inc(sem.m_qb, 1)
-    ve.wait_ge(sem.m_qa, 1)
-    ve.tensor_copy(T.q2s[:, 0:H], T.acc_qa[:, 0:H]).then_inc(sem.c_qa, 1)
-    ve.wait_ge(sem.m_qb, 1)
-    ve.tensor_copy(T.q2s[:, H:R], T.acc_qb[:, 0:H]).then_inc(sem.c_qb, 1)
+    for k in range(NB):
+        te.wait_ge(sem["c_p%d" % k], 1)
+        te.matmul(qbank[k][:, 0:B], T.s[:, :], T.ps[:, k * B:(k + 1) * B], True, True).then_inc(sem["m_q%d" % k], 1)
+    for k in range(NB):
+        ve.wait_ge(sem["m_q%d" % k], 1)
+        ve.tensor_copy(T.q2s[:, k * B:(k + 1) * B], qbank[k][:, 0:B]).then_inc(sem["c_q%d" % k], 1)
 
-    sy.wait_ge(sem.c_pa, 1)
-    sy.dma_start(T.p[:, 0:H], T.ps[:, 0:H]).then_inc(sem.out_a, 16)
-    sc.wait_ge(sem.c_pb, 1)
-    sc.dma_start(T.p[:, H:R], T.ps[:, H:R]).then_inc(sem.out_b, 16)
-    sy.wait_ge(sem.c_qa, 1)
-    sy.dma_start(T.q2[:, 0:H], T.q2s[:, 0:H]).then_inc(sem.out_a, 16)
-    sc.wait_ge(sem.c_qb, 1)
-    sc.dma_start(T.q2[:, H:R], T.q2s[:, H:R]).then_inc(sem.out_b, 16)
+    sy.wait_ge(sem.c_p1, 1)
+    sy.dma_start(T.p[:, 0:2 * B], T.ps[:, 0:2 * B]).then_inc(sem.out_a, 16)
+    sc.wait_ge(sem.c_p3, 1)
+    sc.dma_start(T.p[:, 2 * B:R], T.ps[:, 2 * B:R]).then_inc(sem.out_b, 16)
+    sy.wait_ge(sem.c_q1, 1)
+    sy.dma_start(T.q2[:, 0:2 * B], T.q2s[:, 0:2 * B]).then_inc(sem.out_a, 16)
+    sc.wait_ge(sem.c_q2, 1)
+    sc.dma_start(T.q2[:, 2 * B:3 * B], T.q2s[:, 2 * B:3 * B]).then_inc(sem.out_b, 16)
+    sy.wait_ge(sem.c_q3, 1)
+    sy.dma_start(T.q2[:, 3 * B:R], T.q2s[:, 3 * B:R]).then_inc(sem.out_a, 16)
 
     g.wait_ge(sem.sent, ne)
-    sy.wait_ge(sem.out_a, 32)
+    sy.wait_ge(sem.out_a, 48)
     sc.wait_ge(sem.out_b, 32)

from concourse.bass import DstId, RemoteDMATransfer
from concourse.mybir import AluOpType

W = 128
R = 512
NB = 4
B = R // NB
N = 6

SCRATCH = {
    "land": ("sbuf", [128, N * W], "bfloat16"),
    "qs": ("sbuf", [128, R], "bfloat16"),
    "ones": ("sbuf", [128, W], "bfloat16"),
    "eye": ("sbuf", [128, W], "bfloat16"),
    "st": ("sbuf", [128, W], "bfloat16"),
    "s": ("sbuf", [128, W], "bfloat16"),
    "ps": ("sbuf", [128, R], "bfloat16"),
    "q2s": ("sbuf", [128, R], "bfloat16"),
    "acc_st": ("psum", [128, 512], "float32"),
    "acc_s": ("psum", [128, 512], "float32"),
    "bk0": ("psum", [128, 512], "float32"),
    "bk1": ("psum", [128, 512], "float32"),
    "bk2": ("psum", [128, 512], "float32"),
    "bk3": ("psum", [128, 512], "float32"),
    "bk4": ("psum", [128, 512], "float32"),
    "bk5": ("psum", [128, 512], "float32"),
}
SEMAPHORES = (["ld_mt", "ld_q", "fill", "id", "sent", "m_st", "m_s", "c_st", "c_s", "out_a", "out_b"]
              + ["m_p%d" % k for k in range(NB)] + ["c_p%d" % k for k in range(NB)]
              + ["m_q%d" % k for k in range(NB)] + ["c_q%d" % k for k in range(NB)]
              + ["arr%d" % j for j in range(N)])


def rank_program(g, core, T, topo):
    rank = T.rank_of(core)
    if rank is None:
        return
    n = len(T.cores)
    sem = T.sem
    own = T.land[:, rank * W:(rank + 1) * W]
    te, ve, sy, sc = g.tensor, g.vector, g.sync, g.scalar

    sy.dma_start(own, T.mt[:, :]).then_inc(sem.ld_mt, 16)
    sy.dma_start(T.qs[:, :], T.q[:, :]).then_inc(sem.ld_q, 16)
    ve.memset(T.ones[:, :], 1.0).then_inc(sem.fill, 1)

    peers = [T.cores[(rank + k) % n] for k in range(1, n)]
    mask = topo.mask(core, peers[0])
    for d in peers:
        mask &= topo.mask(core, d)
    ne = bin(mask).count("1")
    ids = []
    for d in peers:
        rid, pid = topo.addr(d, core)
        ids.append(DstId(rid=rid, pnc=pid))
    g.wait_ge(sem.ld_mt, 16)
    g.remote_dma_fused(
        [RemoteDMATransfer(dst_ids=ids, dma_engine_mask=mask, remote_sem=sem["arr%d" % rank],
                           srcs=[own], dsts=[own for _ in peers], alu_op=0)],
        local_sem=sem.sent)

    g.wait_ge(sem.fill, 1)
    g.affine_select(T.eye[:, :], T.ones[:, :], [[-1, W]], AluOpType.is_equal, 0.0, 0, 1).then_inc(sem.id, 1)

    order = [rank] + [(rank - k) % n for k in range(1, n)]
    last = order[-1]
    lastblk = T.land[:, last * W:(last + 1) * W]
    te.wait_ge(sem.id, 1)
    te.wait_ge(sem.ld_mt, 16)
    for i, j in enumerate(order):
        if i > 0:
            te.wait_ge(sem["arr%d" % j], ne)
        blk = T.land[:, j * W:(j + 1) * W]
        if i < n - 1:
            a = te.matmul(T.acc_st[:, 0:W], T.eye[:, :], blk, i == 0, i == n - 2)
            if i == n - 2:
                a.then_inc(sem.m_st, 1)
        b = te.matmul(T.acc_s[:, 0:W], blk, T.eye[:, :], i == 0, i == n - 1)
        if i == n - 1:
            b.then_inc(sem.m_s, 1)

    ve.wait_ge(sem.m_st, 1)
    ve.wait_ge(sem["arr%d" % last], ne)
    ve.tensor_tensor(T.st[:, :], T.acc_st[:, 0:W], lastblk, AluOpType.add).then_inc(sem.c_st, 1)
    ve.wait_ge(sem.m_s, 1)
    ve.tensor_copy(T.s[:, :], T.acc_s[:, 0:W]).then_inc(sem.c_s, 1)

    pbank = [T.bk0, T.bk1, T.bk2, T.bk3]
    qbank = [T.bk4, T.bk5, T.bk0, T.bk1]
    te.wait_ge(sem.c_st, 1)
    te.wait_ge(sem.ld_q, 16)
    for k in range(NB):
        te.matmul(pbank[k][:, 0:B], T.st[:, :], T.qs[:, k * B:(k + 1) * B], True, True).then_inc(sem["m_p%d" % k], 1)
    for k in range(NB):
        ve.wait_ge(sem["m_p%d" % k], 1)
        ve.tensor_copy(T.ps[:, k * B:(k + 1) * B], pbank[k][:, 0:B]).then_inc(sem["c_p%d" % k], 1)
    te.wait_ge(sem.c_s, 1)
    for k in range(NB):
        te.wait_ge(sem["c_p%d" % k], 1)
        te.matmul(qbank[k][:, 0:B], T.s[:, :], T.ps[:, k * B:(k + 1) * B], True, True).then_inc(sem["m_q%d" % k], 1)
    for k in range(NB):
        ve.wait_ge(sem["m_q%d" % k], 1)
        ve.tensor_copy(T.q2s[:, k * B:(k + 1) * B], qbank[k][:, 0:B]).then_inc(sem["c_q%d" % k], 1)

    sy.wait_ge(sem.c_p1, 1)
    sy.dma_start(T.p[:, 0:2 * B], T.ps[:, 0:2 * B]).then_inc(sem.out_a, 16)
    sc.wait_ge(sem.c_p3, 1)
    sc.dma_start(T.p[:, 2 * B:R], T.ps[:, 2 * B:R]).then_inc(sem.out_b, 16)
    sy.wait_ge(sem.c_q1, 1)
    sy.dma_start(T.q2[:, 0:2 * B], T.q2s[:, 0:2 * B]).then_inc(sem.out_a, 16)
    sc.wait_ge(sem.c_q2, 1)
    sc.dma_start(T.q2[:, 2 * B:3 * B], T.q2s[:, 2 * B:3 * B]).then_inc(sem.out_b, 16)
    sy.wait_ge(sem.c_q3, 1)
    sy.dma_start(T.q2[:, 3 * B:R], T.q2s[:, 3 * B:R]).then_inc(sem.out_a, 16)

    g.wait_ge(sem.sent, ne)
    sy.wait_ge(sem.out_a, 48)
    sc.wait_ge(sem.out_b, 32)
